import numpy as np
import ml_dtypes


def mxq(x, axis, fmt="e4m3"):
    dtype, down = {"e4m3": (ml_dtypes.float8_e4m3fn, 7), "e5m2": (ml_dtypes.float8_e5m2, 14)}[fmt]
    v = np.moveaxis(np.asarray(x, np.float32).astype(ml_dtypes.bfloat16).astype(np.float64), axis, -1)
    blocks = v.reshape(v.shape[:-1] + (-1, 32))
    amax = np.abs(blocks).max(-1, keepdims=True)
    byte = np.maximum(np.where(amax > 0, np.frexp(amax)[1] - 1 + 127, 0) - down, 1)
    scale = np.exp2(byte - 127.0)
    codes = (blocks / scale).astype(np.float32).astype(dtype).astype(np.float64)
    return np.moveaxis((codes * scale).reshape(v.shape), -1, axis)


WIDE = False


def mx_kscale(k):
    if not WIDE:
        return np.ones(k)
    levels = np.array([10, -10, 5, -5, 0])
    if k % 512:
        return np.exp2(np.random.permutation(np.resize(levels, k // 32))).repeat(32)
    a = np.empty((k // 512, 16))
    for p in range(k // 512):
        a[p, :8] = np.random.permutation(np.resize(levels, 8))
        for g in range(8):
            far = levels[np.abs(levels - a[p, g]) >= 10]
            a[p, g + 8] = far[np.random.randint(len(far))]
    return np.exp2(a.ravel()).repeat(32)


def f64(x):
    return np.asarray(x).astype(np.float64)


def striped(idx):
    return np.tile(idx.reshape(-1, 16).T, (8, 1)).astype(np.uint16)


def unstriped(offs):
    return offs[:16].T.reshape(-1).astype(np.int64)


E2M1 = np.array([0.0, 0.5, 1.0, 1.5, 2.0, 3.0, 4.0, 6.0, -0.0, -0.5, -1.0, -1.5, -2.0, -3.0, -4.0, -6.0])


def pack_weight(w, fmt):
    k, n = w.shape
    w = f64(np.asarray(w, np.float32).astype(ml_dtypes.bfloat16)).reshape(k // 32, 32, n)
    amax = np.abs(w).max(1)
    if fmt == "e4m3":
        byte = np.frexp(amax)[1] - 1 + 127 - 7
    else:
        mant, ex = np.frexp(amax / 6.0)
        byte = np.where(mant > 0.5, ex, ex - 1) + 127
    byte = np.clip(np.where(amax > 0, byte, 1), 1, 254)
    scaled = (w * np.exp2(127.0 - byte)[:, None, :]).reshape(k, n).astype(np.float32)
    by_word = np.ascontiguousarray(scaled.reshape(k // 512, 128, 4, n).transpose(0, 1, 3, 2))
    if fmt == "e4m3":
        words = by_word.astype(ml_dtypes.float8_e4m3fn).view(np.uint8)
    else:
        c = by_word.astype(ml_dtypes.float4_e2m1fn).view(np.uint8) & 0xF
        words = (c[..., 0::2] | (c[..., 1::2] << 4)).reshape(k // 512, 128, 2 * n)
    return np.ascontiguousarray(words), np.ascontiguousarray(byte.astype(np.uint8).reshape(k // 512, 16, n))


def unpack_weight(words, scales, fmt):
    g, _, n = scales.shape
    words = np.ascontiguousarray(words).reshape(g, 128, n, -1)
    if fmt == "e4m3":
        vals = words.view(ml_dtypes.float8_e4m3fn).astype(np.float64)
    else:
        nib = np.empty((g, 128, n, 4), np.uint8)
        nib[..., 0::2] = words & 0xF
        nib[..., 1::2] = words >> 4
        vals = E2M1[nib]
    vals = vals * np.repeat(np.exp2(scales.astype(np.float64) - 127.0), 8, axis=1)[..., None]
    return vals.transpose(0, 1, 3, 2).reshape(g * 512, n)


def gelu(v):
    return 0.5 * v * (1.0 + np.tanh(np.sqrt(2.0 / np.pi) * (v + 0.044715 * v**3)))


K, T, S, H, P, N = 1024, 2048, 1024, 512, 512, 768

def setup_inputs():
    n = np.random.standard_normal
    s = mx_kscale(K)[:, None]
    u = mx_kscale(H)[:, None]
    tab_words, tab_scales = pack_weight(n((K, T)) * s, "e4m3")
    w1_words, w1_scales = pack_weight(1.1 * n((K, H)) / np.sqrt(K) / s, "e2m1")
    wb_words, wb_scales = pack_weight(n((H, N)) / np.sqrt(H) / u, "e2m1")
    return {
        "tab_words": tab_words, "tab_scales": tab_scales,
        "offs": striped(np.random.permutation(T)[:S]),
        "pos1": striped(np.random.permutation(S)[:P]),
        "pos2": striped(np.random.permutation(S)[:P]),
        "w1_words": w1_words, "w1_scales": w1_scales,
        "w2": (0.55 * n((K, H)) / np.sqrt(K) / s).astype(np.float32),
        "gain": (np.exp(0.3 * n(H)) * u[:, 0]).astype(np.float32),
        "effort": n((H, P)).astype(np.float32),
        "sat": (0.5 * n((H, P)) * u).astype(np.float32),
        "wa": (n((H, N)) / np.sqrt(H) / u).astype(np.float32),
        "wb_words": wb_words, "wb_scales": wb_scales,
        "bo": (0.5 * n(N)).astype(np.float32),
    }

def reference(tab_words, tab_scales, offs, pos1, pos2, w1_words, w1_scales, w2, gain, effort, sat, wa, wb_words, wb_scales, bo):
    v = unpack_weight(tab_words, tab_scales, "e4m3")[:, unstriped(offs)]
    w1 = unpack_weight(w1_words, w1_scales, "e2m1")
    wb = unpack_weight(wb_words, wb_scales, "e2m1")
    level = np.tanh(w1.T @ v)
    phase = np.sin(mxq(f64(w2), 0, "e4m3").T @ v)
    h = (level + phase) * f64(gain)[:, None]
    xa = h[:, unstriped(pos1)] * f64(effort)
    xb = h[:, unstriped(pos2)] + f64(sat)
    y = mxq(f64(wa), 0, "e4m3").T @ mxq(xa, 0, "e4m3") + wb.T @ mxq(xb, 0, "e4m3")
    return y + f64(bo)[:, None]

@@ -1,0 +1,271 @@
+import math
+from contextlib import ExitStack
+
+import concourse.mybir as mybir
+
+K, T, S, H, P, N = 1024, 2048, 1024, 512, 512, 768
+FLOPS = 2 * (2 * K * H * S + 2 * H * N * P)
+
+F32 = mybir.dt.float32
+BF16 = mybir.dt.bfloat16
+I32 = mybir.dt.int32
+U32 = mybir.dt.uint32
+U16 = mybir.dt.uint16
+U8 = mybir.dt.uint8
+FP8X4 = mybir.dt.float8_e4m3fn_x4
+FP4X4 = mybir.dt.float4_e2m1fn_x4
+ALU = mybir.AluOpType
+ACT = mybir.ActivationFunctionType
+
+PARTS = 128
+PACK = 4
+PASSES = K // (PARTS * PACK)
+BANK = 512
+HALVES = S // BANK
+HALF = P // 2
+QUADS = 4
+OUT_TILES = N // PARTS
+ROUNDER = 1.5 * 2.0**23
+
+
+def tile_list_apnoea_watch_scores_kernel(
+    tc, tab_words, tab_scales, offs, pos1, pos2, w1_words, w1_scales, w2, gain, effort, sat, wa, wb_words, wb_scales, bo, out
+):
+    nc = tc.nc
+    with ExitStack() as ctx:
+        keep = ctx.enter_context(tc.tile_pool(name="keep", bufs=1))
+        ring = ctx.enter_context(tc.tile_pool(name="ring", bufs=2))
+        psum = ctx.enter_context(tc.psum_pool(name="psum", bufs=8))
+
+        def held(name, shape, dtype):
+            return keep.tile(shape, dtype, name=name, align_bytes=64)
+
+        def words_of(ap):
+            return ap.bitcast(I32)
+
+        idx = held("idx", [PARTS, S // 16], U16)
+        p1 = held("p1", [PARTS, P // 16], U16)
+        p2 = held("p2", [PARTS, P // 16], U16)
+
+        def shared(tag, shape, dtype):
+            return keep.tile(shape, dtype, name=tag, tag=tag, align_bytes=64)
+
+        tab_w = [shared(f"big{a}", [PARTS, T], I32) for a in range(PASSES)]
+        tab_s = shared("small0", [PARTS, T], U8)
+        w1s_raw = shared("small1", [PARTS, PASSES, H], U8)
+        nc.gpsimd.memset(words_of(w1s_raw[:]), 0)
+        nc.gpsimd.memset(words_of(tab_s[32:64, :]), 0)
+        nc.gpsimd.memset(words_of(tab_s[64:128, :]), 0)
+        planes = held("planes", [PARTS, PASSES, S], U8)
+        nc.gpsimd.memset(words_of(planes[:]), 0)
+
+        nc.sync.dma_start(idx[:], offs)
+        nc.sync.dma_start(words_of(tab_s[0:32, :]), words_of(tab_scales.rearrange("a q t -> q a t")))
+        nc.sync.dma_start(tab_w[0][:], words_of(tab_words[0].rearrange("p t i -> p (t i)")))
+        nc.sync.dma_start(p1[:], pos1)
+        nc.sync.dma_start(p2[:], pos2)
+        nc.sync.dma_start(tab_w[1][:], words_of(tab_words[1].rearrange("p t i -> p (t i)")))
+        w1_raw = shared("small2", [PARTS, PASSES, 2 * H], U8)
+        nc.sync.dma_start(words_of(w1_raw[:]), words_of(w1_words.rearrange("a p c -> p a c")))
+        for q in range(QUADS):
+            nc.sync.dma_start(
+                words_of(w1s_raw[32 * q : 32 * q + 4, :, :]),
+                words_of(w1_scales[:, 4 * q : 4 * q + 4, :].rearrange("a r c -> r a c")),
+            )
+        gains = held("gains", [PARTS, PACK], F32)
+        nc.sync.dma_start(gains[:], gain.rearrange("(p t) -> p t", t=PACK))
+        w2_raw = [shared(f"wide{a}", [PARTS, PACK, H], F32) for a in range(PASSES)]
+        for a in range(PASSES):
+            nc.sync.dma_start(w2_raw[a][:], w2[512 * a : 512 * (a + 1), :].rearrange("(p j) c -> p j c", j=PACK))
+
+        v_s = held("v_s", [PARTS, S], U8)
+        nc.vector.tensor_copy(v_s[:], tab_s[:].indirect(idx[:]))
+        for q in range(QUADS):
+            nc.scalar.dma_start(words_of(planes[32 * q : 32 * q + 4, :, :]), words_of(v_s[8 * q : 8 * q + 8, :]))
+        v_w = [[held(f"v_w{a}{h}", [PARTS, BANK], U32) for h in range(HALVES)] for a in range(PASSES)]
+        w1_w = held("w1_w", [PARTS, PASSES, 2 * H], U8)
+        w1_s = held("w1_s", [PARTS, PASSES, H], U8)
+
+        def gather_words(a, h):
+            nc.vector.tensor_copy(v_w[a][h][:], tab_w[a][:].bitcast(U32).indirect(idx[:, 32 * h : 32 * (h + 1)]))
+
+        gather_words(0, 0)
+        gather_words(0, 1)
+        eff = shared("big0", [PARTS, PACK * P], F32)
+        nc.sync.dma_start(eff[:], effort.rearrange("(p t) j -> p (t j)", t=PACK))
+        gather_words(1, 0)
+        nc.vector.tensor_copy(
+            w1_w[:].bitcast(U16).rearrange("p a (t m) -> p a m t", t=PACK),
+            w1_raw[:].bitcast(U16).rearrange("p a (m t) -> p a m t", t=PACK),
+        )
+        nc.vector.tensor_copy(
+            w1_s[:].rearrange("p a (t m) -> p a m t", t=PACK), w1s_raw[:].rearrange("p a (m t) -> p a m t", t=PACK)
+        )
+        gather_words(1, 1)
+        shift = shared("big1", [PARTS, PACK * P], F32)
+        nc.sync.dma_start(shift[:], sat.rearrange("(p t) j -> p (t j)", t=PACK))
+        wb_w = shared("small2", [PARTS, 2 * N], U8)
+        nc.sync.dma_start(words_of(wb_w[:]), words_of(wb_words[0]))
+        wb_s = shared("small1", [PARTS, N], U8)
+        nc.gpsimd.memset(words_of(wb_s[:]), 0)
+
+        level = [held(f"level{t}", [PARTS, S], F32) for t in range(PACK)]
+        for h in range(HALVES):
+            cols = slice(BANK * h, BANK * (h + 1))
+            for t in range(PACK):
+                acc = psum.tile([PARTS, BANK], F32, name="acc")
+                for a in range(PASSES):
+                    nc.tensor.matmul_mx(
+                        out=acc[:],
+                        lhsT=w1_w[:, a, 2 * PARTS * t : 2 * PARTS * (t + 1)].bitcast(FP4X4),
+                        lhsT_scale=w1_s[:, a, PARTS * t : PARTS * (t + 1)],
+                        rhs=v_w[a][h][:].bitcast(FP8X4),
+                        rhs_scale=planes[:, a, cols],
+                        start=(a == 0),
+                        stop=(a == PASSES - 1),
+                    )
+                nc.scalar.activation(level[t][:, cols], acc[:], ACT.Tanh)
+
+        w2_c = [held(f"w2_c{a}", [PARTS, H], U32) for a in range(PASSES)]
+        w2_s = [held(f"w2_s{a}", [PARTS, H], U8) for a in range(PASSES)]
+        for a in range(PASSES):
+            w2_b = ring.tile([PARTS, H * PACK], BF16, name="w2_b", align_bytes=64)
+            nc.vector.tensor_copy(
+                w2_b[:].rearrange("p (t m j) -> p m j t", t=PACK, j=PACK),
+                w2_raw[a][:].rearrange("p j (m t) -> p m j t", t=PACK),
+            )
+            for lo, hi in ((0, H),) if a < PASSES - 1 else ((0, PARTS), (PARTS, H)):
+                nc.vector.quantize_mx(
+                    out=w2_c[a][:, lo:hi].bitcast(FP8X4), scales=w2_s[a][:, lo:hi], in_=w2_b[:, PACK * lo : PACK * hi]
+                )
+
+        wa_raw = shared("wide0", [PARTS, PACK, N], F32)
+        nc.sync.dma_start(wa_raw[:], wa.rearrange("(p j) n -> p j n", j=PACK))
+        for q in range(QUADS):
+            nc.sync.dma_start(words_of(wb_s[32 * q : 32 * q + 4, :]), words_of(wb_scales[0, 4 * q : 4 * q + 4, :]))
+        bias = shared("wide1", [PARTS, OUT_TILES], F32)
+        with nc.allow_non_contiguous_dma(reason="one bias value a partition and output tile"):
+            nc.sync.dma_start(bias[:], bo.rearrange("(i p) -> p i", p=PARTS))
+
+        xa_f = held("xa_f", [PARTS, PACK, P], F32)
+        feats = [held(f"feats{t}", [PARTS, S], F32) for t in range(PACK)]
+        lg = [shared(f"lg{t}", [PARTS, S], F32) for t in range(PACK)]
+        xb_f = [held("xb_f0", [PARTS, PACK, HALF], F32)]
+        phase = {}
+
+        def front(t):
+            turns = ring.tile([PARTS, S], F32, name="turns")
+            for h in range(HALVES):
+                cols = slice(BANK * h, BANK * (h + 1))
+                acc = psum.tile([PARTS, BANK], F32, name="acc")
+                for a in range(PASSES):
+                    nc.tensor.matmul_mx(
+                        out=acc[:],
+                        lhsT=w2_c[a][:, PARTS * t : PARTS * (t + 1)].bitcast(FP8X4),
+                        lhsT_scale=w2_s[a][:, PARTS * t : PARTS * (t + 1)],
+                        rhs=v_w[a][h][:].bitcast(FP8X4),
+                        rhs_scale=planes[:, a, cols],
+                        start=(a == 0),
+                        stop=(a == PASSES - 1),
+                    )
+                nc.scalar.activation(turns[:, cols], acc[:], ACT.Copy, scale=1.0 / (2.0 * math.pi))
+            whole = ring.tile([PARTS, S], I32, name="whole")
+            nc.vector.tensor_scalar(whole[:], turns[:], ROUNDER, None, ALU.add)
+            rest = ring.tile([PARTS, S], F32, name="rest")
+            nc.vector.scalar_tensor_tensor(rest[:], whole[:], ROUNDER, turns[:], ALU.subtract, ALU.subtract)
+            nc.scalar.activation(lg[t][:], level[t][:], ACT.Copy, scale=gains[:, t : t + 1])
+            phase[t] = ring.tile([PARTS, S], F32, name="phase")
+            nc.scalar.activation(phase[t][:], rest[:], ACT.Sin, scale=-2.0 * math.pi)
+
+        def pick_b(t, h):
+            nc.vector.tensor_tensor(
+                xb_f[h][:, t, :],
+                feats[t][:].indirect(p2[:, 16 * h : 16 * (h + 1)]),
+                shift[:, P * t + HALF * h : P * t + HALF * (h + 1)],
+                ALU.add,
+            )
+
+        def back(t):
+            nc.vector.scalar_tensor_tensor(feats[t][:], phase[t][:], gains[:, t : t + 1], lg[t][:], ALU.mult, ALU.add)
+            nc.vector.tensor_tensor(xa_f[:, t, :], feats[t][:].indirect(p1[:]), eff[:, P * t : P * (t + 1)], ALU.mult)
+            pick_b(t, 0)
+
+        wa_b = held("wa_b", [PARTS, N * PACK], BF16)
+        wa_c = held("wa_c", [PARTS, N], U32)
+        wa_s = held("wa_s", [PARTS, N], U8)
+
+        front(0)
+        for t in range(1, PACK):
+            front(t)
+            back(t - 1)
+        for lo in range(0, N, HALF):
+            part = wa_b[:, PACK * lo : PACK * (lo + HALF)]
+            nc.scalar.copy(
+                part.rearrange("p (c i j) -> p c j i", i=4, j=PACK),
+                wa_raw[:, :, lo : lo + HALF].rearrange("p j (c i) -> p c j i", i=4),
+            )
+            nc.vector.quantize_mx(out=wa_c[:, lo : lo + HALF].bitcast(FP8X4), scales=wa_s[:, lo : lo + HALF], in_=part)
+        back(PACK - 1)
+        xb_f.append(shared(f"lg{PACK - 1}", [PARTS, PACK, HALF], F32))
+
+        def weave(copy, name, source):
+            woven = held(name, [PARTS, HALF * PACK], BF16)
+            copy(woven[:].rearrange("p (c i t) -> p c t i", i=4, t=PACK), source.rearrange("p t (c i) -> p c t i", i=4))
+            return woven
+
+        def quantise(name, woven):
+            codes = held(name + "_c", [PARTS, HALF], U32)
+            scales = held(name + "_s", [PARTS, HALF], U8)
+            nc.vector.quantize_mx(out=codes[:].bitcast(FP8X4), scales=scales[:], in_=woven[:])
+            return codes, scales
+
+        banks = [[psum.tile([PARTS, 2, HALF], F32, name="acc") for k in range(OUT_TILES // 2)] for h in range(2)]
+
+        def product_a(h, codes, scales):
+            for i in range(OUT_TILES):
+                rows = slice(PARTS * i, PARTS * (i + 1))
+                nc.tensor.matmul_mx(
+                    out=banks[h][i // 2][:, i % 2, :],
+                    lhsT=wa_c[:, rows].bitcast(FP8X4),
+                    lhsT_scale=wa_s[:, rows],
+                    rhs=codes[:].bitcast(FP8X4),
+                    rhs_scale=scales[:],
+                    start=(i % 2 == 0),
+                    stop=False,
+                )
+
+        def product_b(h, codes, scales):
+            for k in range(OUT_TILES // 2):
+                scores = held(f"scores{h}{k}", [PARTS, 2, HALF], F32)
+                for e in range(2):
+                    i = 2 * k + e
+                    nc.tensor.matmul_mx(
+                        out=banks[h][k][:, e, :],
+                        lhsT=wb_w[:, 2 * PARTS * i : 2 * PARTS * (i + 1)].bitcast(FP4X4),
+                        lhsT_scale=wb_s[:, PARTS * i : PARTS * (i + 1)],
+                        rhs=codes[:].bitcast(FP8X4),
+                        rhs_scale=scales[:],
+                        start=False,
+                        stop=(e == 1),
+                    )
+                for e in range(2):
+                    i = 2 * k + e
+                    if h == 1 and k != 1:
+                        nc.vector.tensor_scalar(scores[:, e, :], banks[h][k][:, e, :], bias[:, i : i + 1], None, ALU.add)
+                    else:
+                        nc.scalar.activation(scores[:, e, :], banks[h][k][:, e, :], ACT.Identity, bias=bias[:, i : i + 1])
+                nc.sync.dma_start(
+                    out[2 * PARTS * k : 2 * PARTS * (k + 1), HALF * h : HALF * (h + 1)].rearrange("(e p) j -> p e j", p=PARTS),
+                    scores[:],
+                )
+
+        xa_b = [weave(nc.scalar.copy, f"xa_b{h}", xa_f[:, :, HALF * h : HALF * (h + 1)]) for h in range(2)]
+        xb_b0 = weave(nc.scalar.copy, "xb_b0", xb_f[0][:])
+        product_a(0, *quantise("xa0", xa_b[0]))
+        pick_b(0, 1)
+        product_a(1, *quantise("xa1", xa_b[1]))
+        pick_b(1, 1)
+        pick_b(2, 1)
+        product_b(0, *quantise("xb0", xb_b0))
+        pick_b(3, 1)
+        product_b(1, *quantise("xb1", weave(nc.vector.tensor_copy, "xb_b1", xb_f[1][:])))

@@ -35,7 +35,7 @@ def tile_list_apnoea_watch_scores_kernel(
     with ExitStack() as ctx:
         keep = ctx.enter_context(tc.tile_pool(name="keep", bufs=1))
         ring = ctx.enter_context(tc.tile_pool(name="ring", bufs=2))
-        psum = ctx.enter_context(tc.psum_pool(name="psum", bufs=8))
+        psum = ctx.enter_context(tc.psum_pool(name="psum", bufs=2))
 
         def held(name, shape, dtype):
             return keep.tile(shape, dtype, name=name, align_bytes=64)
@@ -52,112 +52,122 @@ def tile_list_apnoea_watch_scores_kernel(
 
         tab_w = [shared(f"big{a}", [PARTS, T], I32) for a in range(PASSES)]
         tab_s = shared("small0", [PARTS, T], U8)
-        w1s_raw = shared("small1", [PARTS, PASSES, H], U8)
-        nc.gpsimd.memset(words_of(w1s_raw[:]), 0)
-        nc.gpsimd.memset(words_of(tab_s[32:64, :]), 0)
-        nc.gpsimd.memset(words_of(tab_s[64:128, :]), 0)
-        planes = held("planes", [PARTS, PASSES, S], U8)
+        w1s_raw = shared("small1", [PARTS, H], U8)
+        warm = held("warm", [PARTS, 1], F32)
+        nc.vector.memset(warm[:], 0.0)
+        nc.scalar.activation(warm[:], warm[:], ACT.Silu)
+        for rows_tile in (w1s_raw, tab_s):
+            nc.vector.memset(words_of(rows_tile[32:64, :]), 0)
+            nc.vector.memset(words_of(rows_tile[64:128, :]), 0)
+        planes = held("planes", [PARTS, PASSES, S + H], U8)
         nc.gpsimd.memset(words_of(planes[:]), 0)
+        gains = held("gains", [PARTS, PACK], F32)
+        nc.gpsimd.dma_start(gains[:], gain.rearrange("(p t) -> p t", t=PACK))
 
         nc.sync.dma_start(idx[:], offs)
+        nc.sync.dma_start(words_of(w1s_raw[0:32, :]), words_of(w1_scales.rearrange("a q c -> q a c")))
         nc.sync.dma_start(words_of(tab_s[0:32, :]), words_of(tab_scales.rearrange("a q t -> q a t")))
+        w1_raw = shared("small3", [PARTS, PASSES, 2 * H], U8)
+        nc.sync.dma_start(words_of(w1_raw[:]), words_of(w1_words.rearrange("a p c -> p a c")))
         nc.sync.dma_start(tab_w[0][:], words_of(tab_words[0].rearrange("p t i -> p (t i)")))
         nc.sync.dma_start(p1[:], pos1)
-        nc.sync.dma_start(p2[:], pos2)
         nc.sync.dma_start(tab_w[1][:], words_of(tab_words[1].rearrange("p t i -> p (t i)")))
-        w1_raw = shared("small2", [PARTS, PASSES, 2 * H], U8)
-        nc.sync.dma_start(words_of(w1_raw[:]), words_of(w1_words.rearrange("a p c -> p a c")))
-        for q in range(QUADS):
-            nc.sync.dma_start(
-                words_of(w1s_raw[32 * q : 32 * q + 4, :, :]),
-                words_of(w1_scales[:, 4 * q : 4 * q + 4, :].rearrange("a r c -> r a c")),
-            )
-        gains = held("gains", [PARTS, PACK], F32)
-        nc.sync.dma_start(gains[:], gain.rearrange("(p t) -> p t", t=PACK))
-        w2_raw = [shared(f"wide{a}", [PARTS, PACK, H], F32) for a in range(PASSES)]
+        w2_raw = [shared(f"wide{a}", [PARTS, PACK * H], F32) for a in range(PASSES)]
         for a in range(PASSES):
-            nc.sync.dma_start(w2_raw[a][:], w2[512 * a : 512 * (a + 1), :].rearrange("(p j) c -> p j c", j=PACK))
+            nc.sync.dma_start(w2_raw[a][:], w2[512 * a : 512 * (a + 1), :].rearrange("(p j) c -> p (j c)", j=PACK))
+        nc.sync.dma_start(p2[:], pos2)
 
+        staged = held("staged", [PARTS, S + H], U8)
+        nc.vector.tensor_copy(
+            staged[:, S:].rearrange("p (t m) -> p m t", t=PACK), w1s_raw[:].rearrange("p (m t) -> p m t", t=PACK)
+        )
         v_s = held("v_s", [PARTS, S], U8)
         nc.vector.tensor_copy(v_s[:], tab_s[:].indirect(idx[:]))
+        nc.vector.tensor_copy(words_of(staged[0:32, 0:S]), words_of(v_s[0:32, :]))
         for q in range(QUADS):
-            nc.scalar.dma_start(words_of(planes[32 * q : 32 * q + 4, :, :]), words_of(v_s[8 * q : 8 * q + 8, :]))
+            nc.scalar.dma_start(words_of(planes[32 * q : 32 * q + 4, :, :]), words_of(staged[8 * q : 8 * q + 8, :]))
         v_w = [[held(f"v_w{a}{h}", [PARTS, BANK], U32) for h in range(HALVES)] for a in range(PASSES)]
-        w1_w = held("w1_w", [PARTS, PASSES, 2 * H], U8)
-        w1_s = held("w1_s", [PARTS, PASSES, H], U8)
+        w1_w = shared("small2", [PARTS, PASSES, 2 * H], U8)
 
         def gather_words(a, h):
             nc.vector.tensor_copy(v_w[a][h][:], tab_w[a][:].bitcast(U32).indirect(idx[:, 32 * h : 32 * (h + 1)]))
 
-        gather_words(0, 0)
-        gather_words(0, 1)
-        eff = shared("big0", [PARTS, PACK * P], F32)
-        nc.sync.dma_start(eff[:], effort.rearrange("(p t) j -> p (t j)", t=PACK))
-        gather_words(1, 0)
         nc.vector.tensor_copy(
             w1_w[:].bitcast(U16).rearrange("p a (t m) -> p a m t", t=PACK),
             w1_raw[:].bitcast(U16).rearrange("p a (m t) -> p a m t", t=PACK),
         )
-        nc.vector.tensor_copy(
-            w1_s[:].rearrange("p a (t m) -> p a m t", t=PACK), w1s_raw[:].rearrange("p a (m t) -> p a m t", t=PACK)
-        )
-        gather_words(1, 1)
-        shift = shared("big1", [PARTS, PACK * P], F32)
+        eff = shared("small3", [PARTS, PACK * P], F32)
+        nc.sync.dma_start(eff[:], effort.rearrange("(p t) j -> p (t j)", t=PACK))
+        gather_words(0, 0)
+        gather_words(0, 1)
+        shift = shared("big0", [PARTS, PACK * P], F32)
         nc.sync.dma_start(shift[:], sat.rearrange("(p t) j -> p (t j)", t=PACK))
-        wb_w = shared("small2", [PARTS, 2 * N], U8)
-        nc.sync.dma_start(words_of(wb_w[:]), words_of(wb_words[0]))
-        wb_s = shared("small1", [PARTS, N], U8)
-        nc.gpsimd.memset(words_of(wb_s[:]), 0)
-
-        level = [held(f"level{t}", [PARTS, S], F32) for t in range(PACK)]
-        for h in range(HALVES):
-            cols = slice(BANK * h, BANK * (h + 1))
-            for t in range(PACK):
-                acc = psum.tile([PARTS, BANK], F32, name="acc")
-                for a in range(PASSES):
-                    nc.tensor.matmul_mx(
-                        out=acc[:],
-                        lhsT=w1_w[:, a, 2 * PARTS * t : 2 * PARTS * (t + 1)].bitcast(FP4X4),
-                        lhsT_scale=w1_s[:, a, PARTS * t : PARTS * (t + 1)],
-                        rhs=v_w[a][h][:].bitcast(FP8X4),
-                        rhs_scale=planes[:, a, cols],
-                        start=(a == 0),
-                        stop=(a == PASSES - 1),
-                    )
-                nc.scalar.activation(level[t][:, cols], acc[:], ACT.Tanh)
+        gather_words(1, 0)
+        gather_words(1, 1)
 
         w2_c = [held(f"w2_c{a}", [PARTS, H], U32) for a in range(PASSES)]
         w2_s = [held(f"w2_s{a}", [PARTS, H], U8) for a in range(PASSES)]
+        w2_b = [shared(("small0", "small1")[a], [PARTS, H * PACK], BF16) for a in range(PASSES)]
         for a in range(PASSES):
-            w2_b = ring.tile([PARTS, H * PACK], BF16, name="w2_b", align_bytes=64)
-            nc.vector.tensor_copy(
-                w2_b[:].rearrange("p (t m j) -> p m j t", t=PACK, j=PACK),
-                w2_raw[a][:].rearrange("p j (m t) -> p m j t", t=PACK),
+            (nc.scalar.copy, nc.vector.tensor_copy)[a](
+                w2_b[a][:].rearrange("p (t m j) -> p m j t", t=PACK, j=PACK),
+                w2_raw[a][:].rearrange("p (j m t) -> p m j t", j=PACK, t=PACK),
             )
+        for a in range(PASSES):
             for lo, hi in ((0, H),) if a < PASSES - 1 else ((0, PARTS), (PARTS, H)):
                 nc.vector.quantize_mx(
-                    out=w2_c[a][:, lo:hi].bitcast(FP8X4), scales=w2_s[a][:, lo:hi], in_=w2_b[:, PACK * lo : PACK * hi]
+                    out=w2_c[a][:, lo:hi].bitcast(FP8X4), scales=w2_s[a][:, lo:hi], in_=w2_b[a][:, PACK * lo : PACK * hi]
                 )
 
-        wa_raw = shared("wide0", [PARTS, PACK, N], F32)
+        def bank(tag, shape):
+            return psum.tile(shape, F32, name=tag, tag=tag, bufs=4 if tag == "acc" else 2)
+
+        level_pairs = [shared("wide0", [PARTS, 2 * S], F32), held("level_pair", [PARTS, 2 * S], F32)]
+        level = [level_pairs[t // 2][:, S * (t % 2) : S * (t % 2 + 1)] for t in range(PACK)]
+
+        def saturate(t, h, tag):
+            cols = slice(BANK * h, BANK * (h + 1))
+            acc = bank(tag, [PARTS, BANK])
+            for a in range(PASSES):
+                nc.tensor.matmul_mx(
+                    out=acc[:],
+                    lhsT=w1_w[:, a, 2 * PARTS * t : 2 * PARTS * (t + 1)].bitcast(FP4X4),
+                    lhsT_scale=planes[:, a, S + PARTS * t : S + PARTS * (t + 1)],
+                    rhs=v_w[a][h][:].bitcast(FP8X4),
+                    rhs_scale=planes[:, a, cols],
+                    start=(a == 0),
+                    stop=(a == PASSES - 1),
+                )
+            nc.scalar.activation(level[t][:, cols], acc[:], ACT.Tanh)
+
+        def weigh(t):
+            nc.scalar.activation(scratch[:], level[t], ACT.Copy, scale=gains[:, t : t + 1])
+
+        scratch = held("scratch", [PARTS, S], F32)
+        for t in range(PACK):
+            saturate(t, 0, "early")
+        saturate(0, 1, "early")
+        weigh(0)
+
+        wa_raw = shared("wide1", [PARTS, PACK, N], F32)
         nc.sync.dma_start(wa_raw[:], wa.rearrange("(p j) n -> p j n", j=PACK))
+        wb_w = shared("small0", [PARTS, 2 * N], U8)
+        nc.sync.dma_start(words_of(wb_w[:]), words_of(wb_words[0]))
+        wb_s = shared("small1", [PARTS, N], U8)
+        nc.gpsimd.memset(words_of(wb_s[:]), 0)
         for q in range(QUADS):
             nc.sync.dma_start(words_of(wb_s[32 * q : 32 * q + 4, :]), words_of(wb_scales[0, 4 * q : 4 * q + 4, :]))
-        bias = shared("wide1", [PARTS, OUT_TILES], F32)
-        with nc.allow_non_contiguous_dma(reason="one bias value a partition and output tile"):
-            nc.sync.dma_start(bias[:], bo.rearrange("(i p) -> p i", p=PARTS))
 
         xa_f = held("xa_f", [PARTS, PACK, P], F32)
         feats = [held(f"feats{t}", [PARTS, S], F32) for t in range(PACK)]
-        lg = [shared(f"lg{t}", [PARTS, S], F32) for t in range(PACK)]
-        xb_f = [held("xb_f0", [PARTS, PACK, HALF], F32)]
+        xb_f = [held("xb_f0", [PARTS, PACK, HALF], F32), scratch[:].rearrange("p (t j) -> p t j", t=PACK)]
         phase = {}
 
         def front(t):
             turns = ring.tile([PARTS, S], F32, name="turns")
             for h in range(HALVES):
                 cols = slice(BANK * h, BANK * (h + 1))
-                acc = psum.tile([PARTS, BANK], F32, name="acc")
+                acc = bank("mid" if t == 0 else "acc", [PARTS, BANK])
                 for a in range(PASSES):
                     nc.tensor.matmul_mx(
                         out=acc[:],
@@ -170,12 +180,12 @@ def tile_list_apnoea_watch_scores_kernel(
                     )
                 nc.scalar.activation(turns[:, cols], acc[:], ACT.Copy, scale=1.0 / (2.0 * math.pi))
             whole = ring.tile([PARTS, S], I32, name="whole")
-            nc.vector.tensor_scalar(whole[:], turns[:], ROUNDER, None, ALU.add)
             rest = ring.tile([PARTS, S], F32, name="rest")
-            nc.vector.scalar_tensor_tensor(rest[:], whole[:], ROUNDER, turns[:], ALU.subtract, ALU.subtract)
-            nc.scalar.activation(lg[t][:], level[t][:], ACT.Copy, scale=gains[:, t : t + 1])
             phase[t] = ring.tile([PARTS, S], F32, name="phase")
-            nc.scalar.activation(phase[t][:], rest[:], ACT.Sin, scale=-2.0 * math.pi)
+            for cols in (slice(0, S),) if t > 0 else (slice(0, BANK), slice(BANK, S)):
+                nc.vector.tensor_scalar(whole[:, cols], turns[:, cols], ROUNDER, None, ALU.add)
+                nc.vector.scalar_tensor_tensor(rest[:, cols], whole[:, cols], ROUNDER, turns[:, cols], ALU.subtract, ALU.subtract)
+                nc.scalar.activation(phase[t][:, cols], rest[:, cols], ACT.Sin, scale=-2.0 * math.pi)
 
         def pick_b(t, h):
             nc.vector.tensor_tensor(
@@ -186,8 +196,14 @@ def tile_list_apnoea_watch_scores_kernel(
             )
 
         def back(t):
-            nc.vector.scalar_tensor_tensor(feats[t][:], phase[t][:], gains[:, t : t + 1], lg[t][:], ALU.mult, ALU.add)
-            nc.vector.tensor_tensor(xa_f[:, t, :], feats[t][:].indirect(p1[:]), eff[:, P * t : P * (t + 1)], ALU.mult)
+            nc.vector.scalar_tensor_tensor(feats[t][:], phase[t][:], gains[:, t : t + 1], scratch[:], ALU.mult, ALU.add)
+            for lo, hi in ((0, P),) if t < PACK - 1 else ((0, HALF), (HALF, P)):
+                nc.vector.tensor_tensor(
+                    xa_f[:, t, lo:hi],
+                    feats[t][:].indirect(p1[:, lo // 16 : hi // 16]),
+                    eff[:, P * t + lo : P * t + hi],
+                    ALU.mult,
+                )
             pick_b(t, 0)
 
         wa_b = held("wa_b", [PARTS, N * PACK], BF16)
@@ -197,7 +213,9 @@ def tile_list_apnoea_watch_scores_kernel(
         front(0)
         for t in range(1, PACK):
             front(t)
+            saturate(t, 1, "mid")
             back(t - 1)
+            weigh(t)
         for lo in range(0, N, HALF):
             part = wa_b[:, PACK * lo : PACK * (lo + HALF)]
             nc.scalar.copy(
@@ -205,21 +223,22 @@ def tile_list_apnoea_watch_scores_kernel(
                 wa_raw[:, :, lo : lo + HALF].rearrange("p j (c i) -> p c j i", i=4),
             )
             nc.vector.quantize_mx(out=wa_c[:, lo : lo + HALF].bitcast(FP8X4), scales=wa_s[:, lo : lo + HALF], in_=part)
+        bias = shared("small2", [PARTS, OUT_TILES], F32)
+        with nc.allow_non_contiguous_dma(reason="one bias value a partition and output tile"):
+            nc.sync.dma_start(bias[:], bo.rearrange("(i p) -> p i", p=PARTS))
         back(PACK - 1)
-        xb_f.append(shared(f"lg{PACK - 1}", [PARTS, PACK, HALF], F32))
 
-        def weave(copy, name, source):
-            woven = held(name, [PARTS, HALF * PACK], BF16)
-            copy(woven[:].rearrange("p (c i t) -> p c t i", i=4, t=PACK), source.rearrange("p t (c i) -> p c t i", i=4))
+        def weave(copy, woven, source):
+            copy(woven.rearrange("p (c i t) -> p c t i", i=4, t=PACK), source.rearrange("p t (c i) -> p c t i", i=4))
             return woven
 
         def quantise(name, woven):
             codes = held(name + "_c", [PARTS, HALF], U32)
             scales = held(name + "_s", [PARTS, HALF], U8)
-            nc.vector.quantize_mx(out=codes[:].bitcast(FP8X4), scales=scales[:], in_=woven[:])
+            nc.vector.quantize_mx(out=codes[:].bitcast(FP8X4), scales=scales[:], in_=woven)
             return codes, scales
 
-        banks = [[psum.tile([PARTS, 2, HALF], F32, name="acc") for k in range(OUT_TILES // 2)] for h in range(2)]
+        banks = [[bank(("early", "mid", "acc")[k], [PARTS, 2, HALF]) for k in range(OUT_TILES // 2)] for h in range(2)]
 
         def product_a(h, codes, scales):
             for i in range(OUT_TILES):
@@ -254,18 +273,16 @@ def tile_list_apnoea_watch_scores_kernel(
                         nc.vector.tensor_scalar(scores[:, e, :], banks[h][k][:, e, :], bias[:, i : i + 1], None, ALU.add)
                     else:
                         nc.scalar.activation(scores[:, e, :], banks[h][k][:, e, :], ACT.Identity, bias=bias[:, i : i + 1])
-                nc.sync.dma_start(
-                    out[2 * PARTS * k : 2 * PARTS * (k + 1), HALF * h : HALF * (h + 1)].rearrange("(e p) j -> p e j", p=PARTS),
-                    scores[:],
-                )
+                    nc.sync.dma_start(out[PARTS * i : PARTS * (i + 1), HALF * h : HALF * (h + 1)], scores[:, e, :])
 
-        xa_b = [weave(nc.scalar.copy, f"xa_b{h}", xa_f[:, :, HALF * h : HALF * (h + 1)]) for h in range(2)]
-        xb_b0 = weave(nc.scalar.copy, "xb_b0", xb_f[0][:])
+        xa_b = [weave(nc.scalar.copy, scratch[:, BANK * h : BANK * (h + 1)].bitcast(BF16), xa_f[:, :, HALF * h : HALF * (h + 1)]) for h in range(2)]
+        xb_b = held("xb_b", [PARTS, HALF * PACK], BF16)
+        weave(nc.scalar.copy, xb_b[:], xb_f[0][:])
         product_a(0, *quantise("xa0", xa_b[0]))
         pick_b(0, 1)
-        product_a(1, *quantise("xa1", xa_b[1]))
         pick_b(1, 1)
+        product_a(1, *quantise("xa1", xa_b[1]))
         pick_b(2, 1)
-        product_b(0, *quantise("xb0", xb_b0))
         pick_b(3, 1)
-        product_b(1, *quantise("xb1", weave(nc.vector.tensor_copy, "xb_b1", xb_f[1][:])))
+        product_b(0, *quantise("xb0", xb_b[:]))
+        product_b(1, *quantise("xb1", weave(nc.vector.tensor_copy, xb_b[:], xb_f[1])))

@@ -67,14 +67,18 @@ def tile_list_apnoea_watch_scores_kernel(
         nc.sync.dma_start(idx[:], offs)
         nc.sync.dma_start(words_of(w1s_raw[0:32, :]), words_of(w1_scales.rearrange("a q c -> q a c")))
         nc.sync.dma_start(words_of(tab_s[0:32, :]), words_of(tab_scales.rearrange("a q t -> q a t")))
-        w1_raw = shared("small3", [PARTS, PASSES, 2 * H], U8)
+        w1_raw = shared("wide1", [PARTS, PASSES, 2 * H], U8)
         nc.sync.dma_start(words_of(w1_raw[:]), words_of(w1_words.rearrange("a p c -> p a c")))
         nc.sync.dma_start(tab_w[0][:], words_of(tab_words[0].rearrange("p t i -> p (t i)")))
         nc.sync.dma_start(p1[:], pos1)
         nc.sync.dma_start(tab_w[1][:], words_of(tab_words[1].rearrange("p t i -> p (t i)")))
-        w2_raw = [shared(f"wide{a}", [PARTS, PACK * H], F32) for a in range(PASSES)]
-        for a in range(PASSES):
+        w2_raw = []
+
+        def load_w2(a):
+            w2_raw.append(shared(f"wide{a}", [PARTS, PACK * H], F32))
             nc.sync.dma_start(w2_raw[a][:], w2[512 * a : 512 * (a + 1), :].rearrange("(p j) c -> p (j c)", j=PACK))
+
+        load_w2(0)
         nc.sync.dma_start(p2[:], pos2)
 
         staged = held("staged", [PARTS, S + H], U8)
@@ -85,7 +89,7 @@ def tile_list_apnoea_watch_scores_kernel(
         nc.vector.tensor_copy(v_s[:], tab_s[:].indirect(idx[:]))
         nc.vector.tensor_copy(words_of(staged[0:32, 0:S]), words_of(v_s[0:32, :]))
         for q in range(QUADS):
-            nc.scalar.dma_start(words_of(planes[32 * q : 32 * q + 4, :, :]), words_of(staged[8 * q : 8 * q + 8, :]))
+            nc.sync.dma_start(words_of(planes[32 * q : 32 * q + 4, :, :]), words_of(staged[8 * q : 8 * q + 8, :]))
         v_w = [[held(f"v_w{a}{h}", [PARTS, BANK], U32) for h in range(HALVES)] for a in range(PASSES)]
         w1_w = shared("small2", [PARTS, PASSES, 2 * H], U8)
 
@@ -96,14 +100,15 @@ def tile_list_apnoea_watch_scores_kernel(
             w1_w[:].bitcast(U16).rearrange("p a (t m) -> p a m t", t=PACK),
             w1_raw[:].bitcast(U16).rearrange("p a (m t) -> p a m t", t=PACK),
         )
-        eff = shared("small3", [PARTS, PACK * P], F32)
-        nc.sync.dma_start(eff[:], effort.rearrange("(p t) j -> p (t j)", t=PACK))
+        load_w2(1)
         gather_words(0, 0)
         gather_words(0, 1)
-        shift = shared("big0", [PARTS, PACK * P], F32)
-        nc.sync.dma_start(shift[:], sat.rearrange("(p t) j -> p (t j)", t=PACK))
+        eff = shared("big0", [PARTS, PACK * P], F32)
+        nc.sync.dma_start(eff[:], effort.rearrange("(p t) j -> p (t j)", t=PACK))
         gather_words(1, 0)
         gather_words(1, 1)
+        shift = shared("big1", [PARTS, PACK * P], F32)
+        nc.sync.dma_start(shift[:], sat.rearrange("(p t) j -> p (t j)", t=PACK))
 
         w2_c = [held(f"w2_c{a}", [PARTS, H], U32) for a in range(PASSES)]
         w2_s = [held(f"w2_s{a}", [PARTS, H], U8) for a in range(PASSES)]
@@ -144,10 +149,10 @@ def tile_list_apnoea_watch_scores_kernel(
             nc.scalar.activation(scratch[:], level[t], ACT.Copy, scale=gains[:, t : t + 1])
 
         scratch = held("scratch", [PARTS, S], F32)
-        for t in range(PACK):
-            saturate(t, 0, "early")
+        saturate(0, 0, "early")
         saturate(0, 1, "early")
         weigh(0)
+        saturate(1, 0, "early")
 
         wa_raw = shared("wide1", [PARTS, PACK, N], F32)
         nc.sync.dma_start(wa_raw[:], wa.rearrange("(p j) n -> p j n", j=PACK))
@@ -213,6 +218,8 @@ def tile_list_apnoea_watch_scores_kernel(
         front(0)
         for t in range(1, PACK):
             front(t)
+            if t > 1:
+                saturate(t, 0, "mid")
             saturate(t, 1, "mid")
             back(t - 1)
             weigh(t)

import math
from contextlib import ExitStack

import concourse.mybir as mybir

K, T, S, H, P, N = 1024, 2048, 1024, 512, 512, 768
FLOPS = 2 * (2 * K * H * S + 2 * H * N * P)

F32 = mybir.dt.float32
BF16 = mybir.dt.bfloat16
I32 = mybir.dt.int32
U32 = mybir.dt.uint32
U16 = mybir.dt.uint16
U8 = mybir.dt.uint8
FP8X4 = mybir.dt.float8_e4m3fn_x4
FP4X4 = mybir.dt.float4_e2m1fn_x4
ALU = mybir.AluOpType
ACT = mybir.ActivationFunctionType

PARTS = 128
PACK = 4
PASSES = K // (PARTS * PACK)
BANK = 512
HALVES = S // BANK
HALF = P // 2
QUADS = 4
OUT_TILES = N // PARTS
ROUNDER = 1.5 * 2.0**23


def tile_list_apnoea_watch_scores_kernel(
    tc, tab_words, tab_scales, offs, pos1, pos2, w1_words, w1_scales, w2, gain, effort, sat, wa, wb_words, wb_scales, bo, out
):
    nc = tc.nc
    with ExitStack() as ctx:
        keep = ctx.enter_context(tc.tile_pool(name="keep", bufs=1))
        ring = ctx.enter_context(tc.tile_pool(name="ring", bufs=2))
        psum = ctx.enter_context(tc.psum_pool(name="psum", bufs=2))

        def held(name, shape, dtype):
            return keep.tile(shape, dtype, name=name, align_bytes=64)

        def words_of(ap):
            return ap.bitcast(I32)

        idx = held("idx", [PARTS, S // 16], U16)
        p1 = held("p1", [PARTS, P // 16], U16)
        p2 = held("p2", [PARTS, P // 16], U16)

        def shared(tag, shape, dtype):
            return keep.tile(shape, dtype, name=tag, tag=tag, align_bytes=64)

        tab_w = [shared(f"big{a}", [PARTS, T], I32) for a in range(PASSES)]
        tab_s = shared("small0", [PARTS, T], U8)
        w1s_raw = shared("small1", [PARTS, H], U8)
        warm = held("warm", [PARTS, 1], F32)
        nc.vector.memset(warm[:], 0.0)
        nc.scalar.activation(warm[:], warm[:], ACT.Silu)
        for rows_tile in (w1s_raw, tab_s):
            nc.vector.memset(words_of(rows_tile[32:64, :]), 0)
            nc.vector.memset(words_of(rows_tile[64:128, :]), 0)
        planes = held("planes", [PARTS, PASSES, S + H], U8)
        nc.gpsimd.memset(words_of(planes[:]), 0)
        gains = held("gains", [PARTS, PACK], F32)
        nc.gpsimd.dma_start(gains[:], gain.rearrange("(p t) -> p t", t=PACK))

        nc.sync.dma_start(idx[:], offs)
        nc.sync.dma_start(words_of(w1s_raw[0:32, :]), words_of(w1_scales.rearrange("a q c -> q a c")))
        nc.sync.dma_start(words_of(tab_s[0:32, :]), words_of(tab_scales.rearrange("a q t -> q a t")))
        w1_raw = shared("wide1", [PARTS, PASSES, 2 * H], U8)
        nc.sync.dma_start(words_of(w1_raw[:]), words_of(w1_words.rearrange("a p c -> p a c")))
        nc.sync.dma_start(tab_w[0][:], words_of(tab_words[0].rearrange("p t i -> p (t i)")))
        nc.sync.dma_start(p1[:], pos1)
        nc.sync.dma_start(tab_w[1][:], words_of(tab_words[1].rearrange("p t i -> p (t i)")))
        w2_raw = []

        def load_w2(a):
            w2_raw.append(shared(f"wide{a}", [PARTS, PACK * H], F32))
            nc.sync.dma_start(w2_raw[a][:], w2[512 * a : 512 * (a + 1), :].rearrange("(p j) c -> p (j c)", j=PACK))

        load_w2(0)
        nc.sync.dma_start(p2[:], pos2)

        staged = held("staged", [PARTS, S + H], U8)
        nc.vector.tensor_copy(
            staged[:, S:].rearrange("p (t m) -> p m t", t=PACK), w1s_raw[:].rearrange("p (m t) -> p m t", t=PACK)
        )
        v_s = held("v_s", [PARTS, S], U8)
        nc.vector.tensor_copy(v_s[:], tab_s[:].indirect(idx[:]))
        nc.vector.tensor_copy(words_of(staged[0:32, 0:S]), words_of(v_s[0:32, :]))
        for q in range(QUADS):
            nc.sync.dma_start(words_of(planes[32 * q : 32 * q + 4, :, :]), words_of(staged[8 * q : 8 * q + 8, :]))
        v_w = [[held(f"v_w{a}{h}", [PARTS, BANK], U32) for h in range(HALVES)] for a in range(PASSES)]
        w1_w = shared("small2", [PARTS, PASSES, 2 * H], U8)

        def gather_words(a, h):
            nc.vector.tensor_copy(v_w[a][h][:], tab_w[a][:].bitcast(U32).indirect(idx[:, 32 * h : 32 * (h + 1)]))

        nc.vector.tensor_copy(
            w1_w[:].bitcast(U16).rearrange("p a (t m) -> p a m t", t=PACK),
            w1_raw[:].bitcast(U16).rearrange("p a (m t) -> p a m t", t=PACK),
        )
        load_w2(1)
        gather_words(0, 0)
        gather_words(0, 1)
        eff = shared("big0", [PARTS, PACK * P], F32)
        nc.sync.dma_start(eff[:], effort.rearrange("(p t) j -> p (t j)", t=PACK))
        gather_words(1, 0)
        gather_words(1, 1)
        shift = shared("big1", [PARTS, PACK * P], F32)
        nc.sync.dma_start(shift[:], sat.rearrange("(p t) j -> p (t j)", t=PACK))

        w2_c = [held(f"w2_c{a}", [PARTS, H], U32) for a in range(PASSES)]
        w2_s = [held(f"w2_s{a}", [PARTS, H], U8) for a in range(PASSES)]
        w2_b = [shared(("small0", "small1")[a], [PARTS, H * PACK], BF16) for a in range(PASSES)]
        for a in range(PASSES):
            (nc.scalar.copy, nc.vector.tensor_copy)[a](
                w2_b[a][:].rearrange("p (t m j) -> p m j t", t=PACK, j=PACK),
                w2_raw[a][:].rearrange("p (j m t) -> p m j t", j=PACK, t=PACK),
            )
        for a in range(PASSES):
            for lo, hi in ((0, H),) if a < PASSES - 1 else ((0, PARTS), (PARTS, H)):
                nc.vector.quantize_mx(
                    out=w2_c[a][:, lo:hi].bitcast(FP8X4), scales=w2_s[a][:, lo:hi], in_=w2_b[a][:, PACK * lo : PACK * hi]
                )

        def bank(tag, shape):
            return psum.tile(shape, F32, name=tag, tag=tag, bufs=4 if tag == "acc" else 2)

        level_pairs = [shared("wide0", [PARTS, 2 * S], F32), held("level_pair", [PARTS, 2 * S], F32)]
        level = [level_pairs[t // 2][:, S * (t % 2) : S * (t % 2 + 1)] for t in range(PACK)]

        def saturate(t, h, tag):
            cols = slice(BANK * h, BANK * (h + 1))
            acc = bank(tag, [PARTS, BANK])
            for a in range(PASSES):
                nc.tensor.matmul_mx(
                    out=acc[:],
                    lhsT=w1_w[:, a, 2 * PARTS * t : 2 * PARTS * (t + 1)].bitcast(FP4X4),
                    lhsT_scale=planes[:, a, S + PARTS * t : S + PARTS * (t + 1)],
                    rhs=v_w[a][h][:].bitcast(FP8X4),
                    rhs_scale=planes[:, a, cols],
                    start=(a == 0),
                    stop=(a == PASSES - 1),
                )
            nc.scalar.activation(level[t][:, cols], acc[:], ACT.Tanh)

        def weigh(t):
            nc.scalar.activation(scratch[:], level[t], ACT.Copy, scale=gains[:, t : t + 1])

        scratch = held("scratch", [PARTS, S], F32)
        saturate(0, 0, "early")
        saturate(0, 1, "early")
        weigh(0)
        saturate(1, 0, "early")

        wa_raw = shared("wide1", [PARTS, PACK, N], F32)
        nc.sync.dma_start(wa_raw[:], wa.rearrange("(p j) n -> p j n", j=PACK))
        wb_w = shared("small0", [PARTS, 2 * N], U8)
        nc.sync.dma_start(words_of(wb_w[:]), words_of(wb_words[0]))
        wb_s = shared("small1", [PARTS, N], U8)
        nc.gpsimd.memset(words_of(wb_s[:]), 0)
        for q in range(QUADS):
            nc.sync.dma_start(words_of(wb_s[32 * q : 32 * q + 4, :]), words_of(wb_scales[0, 4 * q : 4 * q + 4, :]))

        xa_f = held("xa_f", [PARTS, PACK, P], F32)
        feats = [held(f"feats{t}", [PARTS, S], F32) for t in range(PACK)]
        xb_f = [held("xb_f0", [PARTS, PACK, HALF], F32), scratch[:].rearrange("p (t j) -> p t j", t=PACK)]
        phase = {}

        def front(t):
            turns = ring.tile([PARTS, S], F32, name="turns")
            for h in range(HALVES):
                cols = slice(BANK * h, BANK * (h + 1))
                acc = bank("mid" if t == 0 else "acc", [PARTS, BANK])
                for a in range(PASSES):
                    nc.tensor.matmul_mx(
                        out=acc[:],
                        lhsT=w2_c[a][:, PARTS * t : PARTS * (t + 1)].bitcast(FP8X4),
                        lhsT_scale=w2_s[a][:, PARTS * t : PARTS * (t + 1)],
                        rhs=v_w[a][h][:].bitcast(FP8X4),
                        rhs_scale=planes[:, a, cols],
                        start=(a == 0),
                        stop=(a == PASSES - 1),
                    )
                nc.scalar.activation(turns[:, cols], acc[:], ACT.Copy, scale=1.0 / (2.0 * math.pi))
            whole = ring.tile([PARTS, S], I32, name="whole")
            rest = ring.tile([PARTS, S], F32, name="rest")
            phase[t] = ring.tile([PARTS, S], F32, name="phase")
            for cols in (slice(0, S),) if t > 0 else (slice(0, BANK), slice(BANK, S)):
                nc.vector.tensor_scalar(whole[:, cols], turns[:, cols], ROUNDER, None, ALU.add)
                nc.vector.scalar_tensor_tensor(rest[:, cols], whole[:, cols], ROUNDER, turns[:, cols], ALU.subtract, ALU.subtract)
                nc.scalar.activation(phase[t][:, cols], rest[:, cols], ACT.Sin, scale=-2.0 * math.pi)

        def pick_b(t, h):
            nc.vector.tensor_tensor(
                xb_f[h][:, t, :],
                feats[t][:].indirect(p2[:, 16 * h : 16 * (h + 1)]),
                shift[:, P * t + HALF * h : P * t + HALF * (h + 1)],
                ALU.add,
            )

        def back(t):
            nc.vector.scalar_tensor_tensor(feats[t][:], phase[t][:], gains[:, t : t + 1], scratch[:], ALU.mult, ALU.add)
            for lo, hi in ((0, P),) if t < PACK - 1 else ((0, HALF), (HALF, P)):
                nc.vector.tensor_tensor(
                    xa_f[:, t, lo:hi],
                    feats[t][:].indirect(p1[:, lo // 16 : hi // 16]),
                    eff[:, P * t + lo : P * t + hi],
                    ALU.mult,
                )
            pick_b(t, 0)

        wa_b = held("wa_b", [PARTS, N * PACK], BF16)
        wa_c = held("wa_c", [PARTS, N], U32)
        wa_s = held("wa_s", [PARTS, N], U8)

        front(0)
        for t in range(1, PACK):
            front(t)
            if t > 1:
                saturate(t, 0, "mid")
            saturate(t, 1, "mid")
            back(t - 1)
            weigh(t)
        for lo in range(0, N, HALF):
            part = wa_b[:, PACK * lo : PACK * (lo + HALF)]
            nc.scalar.copy(
                part.rearrange("p (c i j) -> p c j i", i=4, j=PACK),
                wa_raw[:, :, lo : lo + HALF].rearrange("p j (c i) -> p c j i", i=4),
            )
            nc.vector.quantize_mx(out=wa_c[:, lo : lo + HALF].bitcast(FP8X4), scales=wa_s[:, lo : lo + HALF], in_=part)
        bias = shared("small2", [PARTS, OUT_TILES], F32)
        with nc.allow_non_contiguous_dma(reason="one bias value a partition and output tile"):
            nc.sync.dma_start(bias[:], bo.rearrange("(i p) -> p i", p=PARTS))
        back(PACK - 1)

        def weave(copy, woven, source):
            copy(woven.rearrange("p (c i t) -> p c t i", i=4, t=PACK), source.rearrange("p t (c i) -> p c t i", i=4))
            return woven

        def quantise(name, woven):
            codes = held(name + "_c", [PARTS, HALF], U32)
            scales = held(name + "_s", [PARTS, HALF], U8)
            nc.vector.quantize_mx(out=codes[:].bitcast(FP8X4), scales=scales[:], in_=woven)
            return codes, scales

        banks = [[bank(("early", "mid", "acc")[k], [PARTS, 2, HALF]) for k in range(OUT_TILES // 2)] for h in range(2)]

        def product_a(h, codes, scales):
            for i in range(OUT_TILES):
                rows = slice(PARTS * i, PARTS * (i + 1))
                nc.tensor.matmul_mx(
                    out=banks[h][i // 2][:, i % 2, :],
                    lhsT=wa_c[:, rows].bitcast(FP8X4),
                    lhsT_scale=wa_s[:, rows],
                    rhs=codes[:].bitcast(FP8X4),
                    rhs_scale=scales[:],
                    start=(i % 2 == 0),
                    stop=False,
                )

        def product_b(h, codes, scales):
            for k in range(OUT_TILES // 2):
                scores = held(f"scores{h}{k}", [PARTS, 2, HALF], F32)
                for e in range(2):
                    i = 2 * k + e
                    nc.tensor.matmul_mx(
                        out=banks[h][k][:, e, :],
                        lhsT=wb_w[:, 2 * PARTS * i : 2 * PARTS * (i + 1)].bitcast(FP4X4),
                        lhsT_scale=wb_s[:, PARTS * i : PARTS * (i + 1)],
                        rhs=codes[:].bitcast(FP8X4),
                        rhs_scale=scales[:],
                        start=False,
                        stop=(e == 1),
                    )
                for e in range(2):
                    i = 2 * k + e
                    if h == 1 and k != 1:
                        nc.vector.tensor_scalar(scores[:, e, :], banks[h][k][:, e, :], bias[:, i : i + 1], None, ALU.add)
                    else:
                        nc.scalar.activation(scores[:, e, :], banks[h][k][:, e, :], ACT.Identity, bias=bias[:, i : i + 1])
                    nc.sync.dma_start(out[PARTS * i : PARTS * (i + 1), HALF * h : HALF * (h + 1)], scores[:, e, :])

        xa_b = [weave(nc.scalar.copy, scratch[:, BANK * h : BANK * (h + 1)].bitcast(BF16), xa_f[:, :, HALF * h : HALF * (h + 1)]) for h in range(2)]
        xb_b = held("xb_b", [PARTS, HALF * PACK], BF16)
        weave(nc.scalar.copy, xb_b[:], xb_f[0][:])
        product_a(0, *quantise("xa0", xa_b[0]))
        pick_b(0, 1)
        pick_b(1, 1)
        product_a(1, *quantise("xa1", xa_b[1]))
        pick_b(2, 1)
        pick_b(3, 1)
        product_b(0, *quantise("xb0", xb_b[:]))
        product_b(1, *quantise("xb1", weave(nc.vector.tensor_copy, xb_b[:], xb_f[1])))
